import numpy as np
import ml_dtypes


def mxq(x, axis, fmt="e4m3"):
    dtype, down = {"e4m3": (ml_dtypes.float8_e4m3fn, 7), "e5m2": (ml_dtypes.float8_e5m2, 14)}[fmt]
    v = np.moveaxis(np.asarray(x, np.float32).astype(ml_dtypes.bfloat16).astype(np.float64), axis, -1)
    blocks = v.reshape(v.shape[:-1] + (-1, 32))
    amax = np.abs(blocks).max(-1, keepdims=True)
    byte = np.maximum(np.where(amax > 0, np.frexp(amax)[1] - 1 + 127, 0) - down, 1)
    scale = np.exp2(byte - 127.0)
    codes = (blocks / scale).astype(np.float32).astype(dtype).astype(np.float64)
    return np.moveaxis((codes * scale).reshape(v.shape), -1, axis)


WIDE = False


def mx_kscale(k):
    if not WIDE:
        return np.ones(k)
    levels = np.array([10, -10, 5, -5, 0])
    if k % 512:
        return np.exp2(np.random.permutation(np.resize(levels, k // 32))).repeat(32)
    a = np.empty((k // 512, 16))
    for p in range(k // 512):
        a[p, :8] = np.random.permutation(np.resize(levels, 8))
        for g in range(8):
            far = levels[np.abs(levels - a[p, g]) >= 10]
            a[p, g + 8] = far[np.random.randint(len(far))]
    return np.exp2(a.ravel()).repeat(32)


def f64(x):
    return np.asarray(x).astype(np.float64)


def striped(idx):
    return np.tile(idx.reshape(-1, 16).T, (8, 1)).astype(np.uint16)


def unstriped(offs):
    return offs[:16].T.reshape(-1).astype(np.int64)


def striped8(idx):
    return np.concatenate([x.reshape(-1, 16).T for x in idx]).astype(np.uint16)


def runs(offs, k):
    lists = np.stack([offs[16 * r : 16 * r + 16].T.reshape(-1) for r in range(8)]).astype(np.int64)
    return lists[np.arange(k) % 512 // 64]


def pack_weight(w):
    k, n = w.shape
    w = f64(np.asarray(w, np.float32).astype(ml_dtypes.bfloat16)).reshape(k // 32, 32, n)
    amax = np.abs(w).max(1)
    byte = np.clip(np.where(amax > 0, np.frexp(amax)[1] - 1 + 127 - 7, 1), 1, 254)
    scaled = (w * np.exp2(127.0 - byte)[:, None, :]).reshape(k, n).astype(np.float32)
    words = np.ascontiguousarray(scaled.reshape(k // 512, 128, 4, n).transpose(0, 1, 3, 2)).astype(ml_dtypes.float8_e4m3fn).view(np.uint8)
    return words, np.ascontiguousarray(byte.astype(np.uint8).reshape(k // 512, 16, n))


def unpack_weight(words, scales):
    g, p, n, _ = words.shape
    vals = np.ascontiguousarray(words).view(ml_dtypes.float8_e4m3fn).astype(np.float64) * np.repeat(np.exp2(scales.astype(np.float64) - 127.0), 8, axis=1)[..., None]
    return vals.transpose(0, 1, 3, 2).reshape(g * 512, n)


def sigmoid(v):
    return 1.0 / (1.0 + np.exp(-np.maximum(v, -700.0)))


K, T, S, H, W, G = 512, 2048, 512, 512, 256, 2048


def setup_inputs():
    n = np.random.standard_normal
    s = mx_kscale(K)[:, None]
    packed_xT = pack_weight(n((K, T)) * s)
    packed_dT = pack_weight(n((K, G)) / s)
    perm = np.stack([np.random.permutation(S) for _ in range(8)])
    return {
        "x_words": packed_xT[0],
        "x_scales": packed_xT[1],
        "w1": (n((K, H)) / np.sqrt(K) / s).astype(np.float32),
        "gs": (np.random.uniform(0.5, 1.5, (K, 1)) * s).astype(np.float32),
        "d_words": packed_dT[0],
        "d_scales": packed_dT[1],
        "sl": np.random.uniform(1.0, 2.0, (H, 1)).astype(np.float32),
        "th": (0.5 * n((H, 1))).astype(np.float32),
        "offs": striped(np.random.permutation(T)[:S]),
        "n1": striped8(perm[:, :W]),
        "n2": striped8(perm[:, W:]),
        "ka": striped8(np.random.randint(0, G, (8, H))),
        "kb": striped8(np.random.randint(0, G, (8, H))),
        "n3": striped8(np.stack([np.random.permutation(S) for _ in range(8)])),
    }


def reference(x_words, x_scales, w1, gs, d_words, d_scales, sl, th, offs, n1, n2, ka, kb, n3):
    d_ka = unpack_weight(d_words, d_scales)[np.arange(K)[:, None], runs(ka, K)]
    xq = unpack_weight(x_words, x_scales)[:, unstriped(offs)]
    y = mxq(f64(w1), 0, "e4m3").T @ xq
    pb = y[np.arange(H)[:, None], runs(n2, H)]
    pa = y[np.arange(H)[:, None], runs(n1, H)]
    rb = pb - (0.5 * pa)
    ra = np.sqrt((pa) ** 2 + (pb) ** 2 + 0.25)
    ds = np.zeros((H, S))
    ds[np.arange(H)[:, None], runs(n1, H)] = ra
    dt = ds.copy()
    dt[np.arange(H)[:, None], runs(n2, H)] = rb
    z = f64(gs) * dt
    zq = mxq(z, 0, "e4m3")
    d_kb = unpack_weight(d_words, d_scales)[np.arange(K)[:, None], runs(kb, K)]
    h = 0.0625 * (d_ka.T @ zq + d_kb.T @ zq)
    sg = sigmoid(f64(sl) * (h[np.arange(H)[:, None], runs(n3, H)] - f64(th)))
    return h * sg

@@ -1,0 +1,151 @@
+from contextlib import ExitStack
+
+import concourse.mybir as mybir
+
+K, T, S, H, W, G = 512, 2048, 512, 512, 256, 2048
+P, PACK = 128, 4
+FLOPS = 2 * K * H * S * 3
+
+F32 = mybir.dt.float32
+BF16 = mybir.dt.bfloat16
+I32 = mybir.dt.int32
+U32 = mybir.dt.uint32
+U16 = mybir.dt.uint16
+U8 = mybir.dt.uint8
+FP8X4 = mybir.dt.float8_e4m3fn_x4
+ACT = mybir.ActivationFunctionType
+ALU = mybir.AluOpType
+
+
+def tile_picked_daqpolaresa_none_p_kernel(tc, x_words, x_scales, w1, gs, d_words, d_scales, sl, th, offs, n1, n2, ka, kb, n3, out):
+    nc = tc.nc
+    with ExitStack() as ctx:
+        lists = ctx.enter_context(tc.tile_pool(name="lists", bufs=1))
+        keep = ctx.enter_context(tc.tile_pool(name="keep", bufs=1))
+        psum = ctx.enter_context(tc.psum_pool(name="psum", bufs=1))
+
+        def load_list(src, name):
+            tile = lists.tile(list(src.shape), U16, name=name)
+            nc.sync.dma_start(tile[:], src)
+            return tile
+
+        def load_rows(src, name):
+            tile = keep.tile([P, PACK], F32, name=name)
+            nc.gpsimd.dma_start(tile[:], src.rearrange("(p t) o -> p (t o)", t=PACK))
+            return tile
+
+        xs_tab = keep.tile([P, T], U8, name="xs_tab")
+        ds_tab = keep.tile([P, G], U8, name="ds_tab")
+        ds_plane = keep.tile([P, 2 * H], U8, name="ds_plane", align_bytes=64)
+        quarter = keep.tile([P, 1], F32, name="quarter")
+        nc.vector.memset(xs_tab[:].bitcast(I32), 0)
+        nc.vector.memset(ds_tab[:].bitcast(I32), 0)
+        nc.gpsimd.memset(ds_plane[:].bitcast(I32), 0)
+        nc.gpsimd.memset(quarter[:], 0.25)
+
+        w_raw = [keep.tile([P, PACK, H // 2], F32, name=f"w_raw{c}") for c in range(2)]
+        w_view = w1.rearrange("(p j) i -> p j i", j=PACK)
+        for c in range(2):
+            nc.sync.dma_start(w_raw[c][:], w_view[:, :, c * (H // 2) : (c + 1) * (H // 2)])
+        offs_l = load_list(offs, "offs_l")
+        for q in range(4):
+            nc.scalar.dma_start(xs_tab[32 * q : 32 * q + 4, :].bitcast(I32), x_scales[0, 4 * q : 4 * q + 4, :].bitcast(I32))
+        xw_tab = keep.tile([P, T], I32, name="xw_tab")
+        nc.sync.dma_start(xw_tab[:], x_words[0].rearrange("p n t -> p (n t)").bitcast(I32))
+        ka_l = load_list(ka, "ka_l")
+        kb_l = load_list(kb, "kb_l")
+        for r in range(2):
+            nc.scalar.dma_start(ds_tab[r:P:16, :].bitcast(I32), d_scales[0, r:16:2, :].bitcast(I32))
+        n1_l = load_list(n1, "n1_l")
+        n2_l = load_list(n2, "n2_l")
+        dw_tab = keep.tile([P, G], I32, name="dw_tab")
+        nc.sync.dma_start(dw_tab[:], d_words[0].rearrange("p n t -> p (n t)").bitcast(I32))
+        n3_l = load_list(n3, "n3_l")
+        gs_t = load_rows(gs, "gs_t")
+        sl_t = load_rows(sl, "sl_t")
+        th_t = load_rows(th, "th_t")
+
+        xs_g = keep.tile([P, S], U8, name="xs_g", align_bytes=64)
+        nc.vector.tensor_copy(xs_g[:], xs_tab[:].indirect(offs_l[:]))
+        w_bf = keep.tile([P, H * PACK], BF16, name="w_bf", align_bytes=64)
+        w_bf_v = w_bf[:].rearrange("p (t m j) -> p m t j", t=PACK, j=PACK)
+        nc.scalar.copy(w_bf_v[:, 0:64], w_raw[0][:].rearrange("p j (m t) -> p m t j", t=PACK))
+        nc.vector.tensor_copy(w_bf_v[:, 64:128], w_raw[1][:].rearrange("p j (m t) -> p m t j", t=PACK))
+        w_q = keep.tile([P, H], U32, name="w_q", align_bytes=64)
+        w_s = keep.tile([P, H], U8, name="w_s", align_bytes=64)
+        nc.vector.quantize_mx(out=w_q[:].bitcast(FP8X4), scales=w_s[:], in_=w_bf[:])
+        xw_g = keep.tile([P, S], U32, name="xw_g", align_bytes=64)
+        nc.vector.tensor_copy(xw_g[:], xw_tab[:].bitcast(U32).indirect(offs_l[:]))
+
+        y_ps = [psum.tile([P, S], F32, name=f"y_ps{t}") for t in range(PACK)]
+        for t in range(PACK):
+            cols = slice(t * P, (t + 1) * P)
+            nc.tensor.matmul_mx(out=y_ps[t][:], lhsT=w_q[:, cols].bitcast(FP8X4), lhsT_scale=w_s[:, cols],
+                                rhs=xw_g[:].bitcast(FP8X4), rhs_scale=xs_g[:], start=True, stop=True)
+
+        ds_g = keep.tile([P, 2 * H], U8, name="ds_g")
+        dw_g = keep.tile([P, 2 * H], U32, name="dw_g")
+        for a, lst in enumerate((ka_l, kb_l)):
+            nc.vector.tensor_copy(ds_g[:, a * H : (a + 1) * H], ds_tab[:].indirect(lst[:]))
+        ds_dealt = keep.tile([P, 2 * H], U8, name="ds_dealt")
+        nc.vector.tensor_copy(ds_dealt[:].rearrange("p (a t m) -> p a t m", a=2, t=PACK),
+                              ds_g[:].rearrange("p (a m t) -> p a t m", a=2, t=PACK))
+        for r in range(4):
+            src = 16 * (r // 2) + r % 2
+            nc.sync.dma_start(ds_plane[r:P:32, :].bitcast(I32), ds_dealt[src:P:32, :].bitcast(I32))
+        for a, lst in enumerate((ka_l, kb_l)):
+            nc.vector.tensor_copy(dw_g[:, a * H : (a + 1) * H], dw_tab[:].bitcast(U32).indirect(lst[:]))
+        dw_dealt = keep.tile([P, 2 * H], U32, name="dw_dealt", align_bytes=64)
+        nc.vector.tensor_copy(dw_dealt[:].rearrange("p (a t m) -> p a m t", a=2, t=PACK),
+                              dw_g[:].rearrange("p (a m t) -> p a m t", a=2, t=PACK))
+        nbias = keep.tile([P, PACK], F32, name="nbias")
+        nc.vector.scalar_tensor_tensor(nbias[:], sl_t[:], -1.0, th_t[:], ALU.mult, ALU.mult)
+
+        z_planes = keep.tile([P, PACK, S], BF16, name="z_planes")
+        for t in range(PACK):
+            y = keep.tile([P, S], F32, name=f"y{t}")
+            nc.scalar.copy(y[:], y_ps[t][:])
+            pah = keep.tile([P, W], F32, name=f"pah{t}")
+            pb = keep.tile([P, W], F32, name=f"pb{t}")
+            nc.scalar.activation(pah[:], y[:].indirect(n1_l[:]), ACT.Copy, scale=-0.5)
+            nc.scalar.activation(pb[:], y[:].indirect(n2_l[:]), ACT.Copy)
+            dt = keep.tile([P, S], F32, name=f"dt{t}")
+            nc.vector.tensor_tensor(dt[:].indirect(n2_l[:]), pb[:], pah[:], ALU.add)
+            a2 = keep.tile([P, W], F32, name=f"a2{t}")
+            b2 = keep.tile([P, W], F32, name=f"b2{t}")
+            nc.scalar.activation(a2[:], pah[:], ACT.Square, scale=2.0)
+            nc.scalar.activation(b2[:], pb[:], ACT.Square)
+            ss = keep.tile([P, W], F32, name=f"ss{t}")
+            nc.vector.tensor_tensor(ss[:], a2[:], b2[:], ALU.add)
+            ra = keep.tile([P, W], F32, name=f"ra{t}")
+            nc.scalar.activation(ra[:], ss[:], ACT.Sqrt, bias=quarter[:])
+            nc.vector.tensor_copy(dt[:].indirect(n1_l[:]), ra[:])
+            if t < PACK - 1:
+                nc.scalar.activation(z_planes[:, t, :], dt[:], ACT.Copy, scale=gs_t[:, t : t + 1])
+            else:
+                nc.vector.tensor_scalar(z_planes[:, t, :], dt[:], gs_t[:, t : t + 1], None, ALU.mult)
+
+        z_bf = keep.tile([P, S * PACK], BF16, name="z_bf", align_bytes=64)
+        nc.vector.tensor_copy(z_bf[:].rearrange("p (c i t) -> p c t i", i=4, t=PACK),
+                              z_planes[:].rearrange("p t (c i) -> p c t i", i=4))
+        z_q = keep.tile([P, S], U32, name="z_q", align_bytes=64)
+        z_s = keep.tile([P, S], U8, name="z_s", align_bytes=64)
+        nc.vector.quantize_mx(out=z_q[:].bitcast(FP8X4), scales=z_s[:], in_=z_bf[:])
+
+        out_v = out.rearrange("(p t) j -> t p j", t=PACK)
+        for t in range(PACK):
+            h_ps = psum.tile([P, S], F32, name=f"h_ps{t}")
+            for a in range(2):
+                cols = slice(a * H + t * P, a * H + (t + 1) * P)
+                nc.tensor.matmul_mx(out=h_ps[:], lhsT=dw_dealt[:, cols].bitcast(FP8X4), lhsT_scale=ds_plane[:, cols],
+                                    rhs=z_q[:].bitcast(FP8X4), rhs_scale=z_s[:], start=(a == 0), stop=(a == 1))
+            h = keep.tile([P, S], F32, name=f"h{t}")
+            nc.vector.tensor_scalar(h[:], h_ps[:], 0.0625, None, ALU.mult)
+            sg = keep.tile([P, S], F32, name=f"sg{t}")
+            res = keep.tile([P, S], F32, name=f"res{t}")
+            for c in range(2):
+                cols = slice(c * W, (c + 1) * W)
+                nc.scalar.activation(sg[:, cols], h[:].indirect(n3_l[:, c * 16 : (c + 1) * 16]), ACT.Sigmoid,
+                                     bias=nbias[:, t : t + 1], scale=sl_t[:, t : t + 1])
+            nc.vector.tensor_tensor(res[:], h[:], sg[:], ALU.mult)
+            nc.sync.dma_start(out_v[t], res[:])

@@ -4,6 +4,9 @@ import concourse.mybir as mybir
 
 K, T, S, H, W, G = 512, 2048, 512, 512, 256, 2048
 P, PACK = 128, 4
+M_SCALAR = 48
+J_SCALAR = 128
+ORDER = (1, 2, 3, 0)
 FLOPS = 2 * K * H * S * 3
 
 F32 = mybir.dt.float32
@@ -31,57 +34,91 @@ def tile_picked_daqpolaresa_none_p_kernel(tc, x_words, x_scales, w1, gs, d_words
 
         def load_rows(src, name):
             tile = keep.tile([P, PACK], F32, name=name)
-            nc.gpsimd.dma_start(tile[:], src.rearrange("(p t) o -> p (t o)", t=PACK))
+            nc.sync.dma_start(tile[:], src.rearrange("(p t) o -> p (t o)", t=PACK))
             return tile
 
         xs_tab = keep.tile([P, T], U8, name="xs_tab")
         ds_tab = keep.tile([P, G], U8, name="ds_tab")
         ds_plane = keep.tile([P, 2 * H], U8, name="ds_plane", align_bytes=64)
         quarter = keep.tile([P, 1], F32, name="quarter")
-        nc.vector.memset(xs_tab[:].bitcast(I32), 0)
         nc.vector.memset(ds_tab[:].bitcast(I32), 0)
-        nc.gpsimd.memset(ds_plane[:].bitcast(I32), 0)
-        nc.gpsimd.memset(quarter[:], 0.25)
+        nc.gpsimd.memset(xs_tab[:].bitcast(I32), 0)
 
-        w_raw = [keep.tile([P, PACK, H // 2], F32, name=f"w_raw{c}") for c in range(2)]
-        w_view = w1.rearrange("(p j) i -> p j i", j=PACK)
-        for c in range(2):
-            nc.sync.dma_start(w_raw[c][:], w_view[:, :, c * (H // 2) : (c + 1) * (H // 2)])
-        offs_l = load_list(offs, "offs_l")
-        for q in range(4):
-            nc.scalar.dma_start(xs_tab[32 * q : 32 * q + 4, :].bitcast(I32), x_scales[0, 4 * q : 4 * q + 4, :].bitcast(I32))
-        xw_tab = keep.tile([P, T], I32, name="xw_tab")
-        nc.sync.dma_start(xw_tab[:], x_words[0].rearrange("p n t -> p (n t)").bitcast(I32))
         ka_l = load_list(ka, "ka_l")
         kb_l = load_list(kb, "kb_l")
-        for r in range(2):
-            nc.scalar.dma_start(ds_tab[r:P:16, :].bitcast(I32), d_scales[0, r:16:2, :].bitcast(I32))
-        n1_l = load_list(n1, "n1_l")
-        n2_l = load_list(n2, "n2_l")
+        nc.sync.dma_start(ds_tab[0:P:8, :].bitcast(I32), d_scales[0].bitcast(I32))
+        w_raw = keep.tile([P, PACK, H], F32, name="w_raw")
+        nc.sync.dma_start(w_raw[:], w1.rearrange("(p j) i -> p j i", j=PACK))
+        offs_l = load_list(offs, "offs_l")
+        for q in range(4):
+            nc.sync.dma_start(xs_tab[32 * q : 32 * q + 4, :].bitcast(I32), x_scales[0, 4 * q : 4 * q + 4, :].bitcast(I32))
+        xw_tab = keep.tile([P, T], I32, name="xw_tab")
+        nc.sync.dma_start(xw_tab[:], x_words[0].rearrange("p n t -> p (n t)").bitcast(I32))
         dw_tab = keep.tile([P, G], I32, name="dw_tab")
         nc.sync.dma_start(dw_tab[:], d_words[0].rearrange("p n t -> p (n t)").bitcast(I32))
-        n3_l = load_list(n3, "n3_l")
+        n1_l = load_list(n1, "n1_l")
+        n2_l = load_list(n2, "n2_l")
         gs_t = load_rows(gs, "gs_t")
         sl_t = load_rows(sl, "sl_t")
         th_t = load_rows(th, "th_t")
+        n3_l = load_list(n3, "n3_l")
+        nc.gpsimd.memset(quarter[:], 0.25)
+        nc.gpsimd.memset(ds_plane[:].bitcast(I32), 0)
 
         xs_g = keep.tile([P, S], U8, name="xs_g", align_bytes=64)
         nc.vector.tensor_copy(xs_g[:], xs_tab[:].indirect(offs_l[:]))
         w_bf = keep.tile([P, H * PACK], BF16, name="w_bf", align_bytes=64)
         w_bf_v = w_bf[:].rearrange("p (t m j) -> p m t j", t=PACK, j=PACK)
-        nc.scalar.copy(w_bf_v[:, 0:64], w_raw[0][:].rearrange("p j (m t) -> p m t j", t=PACK))
-        nc.vector.tensor_copy(w_bf_v[:, 64:128], w_raw[1][:].rearrange("p j (m t) -> p m t j", t=PACK))
+        w_raw_v = w_raw[:].rearrange("p j (m t) -> p m t j", t=PACK)
+        nc.scalar.activation(w_bf_v[:, 0:M_SCALAR], w_raw_v[:, 0:M_SCALAR], ACT.Copy)
+        nc.vector.tensor_copy(w_bf_v[:, M_SCALAR:P], w_raw_v[:, M_SCALAR:P])
         w_q = keep.tile([P, H], U32, name="w_q", align_bytes=64)
         w_s = keep.tile([P, H], U8, name="w_s", align_bytes=64)
         nc.vector.quantize_mx(out=w_q[:].bitcast(FP8X4), scales=w_s[:], in_=w_bf[:])
         xw_g = keep.tile([P, S], U32, name="xw_g", align_bytes=64)
         nc.vector.tensor_copy(xw_g[:], xw_tab[:].bitcast(U32).indirect(offs_l[:]))
 
-        y_ps = [psum.tile([P, S], F32, name=f"y_ps{t}") for t in range(PACK)]
-        for t in range(PACK):
+        y_ps = [psum.tile([P, S], F32, name=f"y_ps{t}", tag=f"bank{t}") for t in range(PACK)]
+        for t in ORDER:
             cols = slice(t * P, (t + 1) * P)
             nc.tensor.matmul_mx(out=y_ps[t][:], lhsT=w_q[:, cols].bitcast(FP8X4), lhsT_scale=w_s[:, cols],
                                 rhs=xw_g[:].bitcast(FP8X4), rhs_scale=xs_g[:], start=True, stop=True)
+
+        z_bf = keep.tile([P, S * PACK], BF16, name="z_bf", align_bytes=64)
+        z_v = z_bf[:].rearrange("p (j t) -> p t j", t=PACK)
+        y, pah, pb, a2, b2, ss, ra, dt = ([keep.tile([P, n], F32, name=f"{name}{t}") for t in range(PACK)]
+            for name, n in (("y", S), ("pah", W), ("pb", W), ("a2", W), ("b2", W), ("ss", W), ("ra", W), ("dt", S)))
+
+        def fetch(t):
+            nc.scalar.copy(y[t][:], y_ps[t][:])
+            nc.scalar.activation(pah[t][:], y[t][:].indirect(n1_l[:]), ACT.Copy, scale=-0.5)
+            nc.scalar.activation(pb[t][:], y[t][:].indirect(n2_l[:]), ACT.Copy)
+            nc.vector.tensor_tensor(dt[t][:].indirect(n2_l[:]), pb[t][:], pah[t][:], ALU.add)
+
+        def squares(t):
+            nc.scalar.activation(a2[t][:], pah[t][:], ACT.Square, scale=2.0)
+            nc.scalar.activation(b2[t][:], pb[t][:], ACT.Square)
+            nc.vector.tensor_tensor(ss[t][:], a2[t][:], b2[t][:], ALU.add)
+
+        def root(t):
+            nc.scalar.activation(ra[t][:], ss[t][:], ACT.Sqrt, bias=quarter[:])
+            nc.vector.tensor_copy(dt[t][:].indirect(n1_l[:]), ra[t][:])
+
+        def weigh(t):
+            split = J_SCALAR if t == ORDER[-1] else S
+            nc.scalar.activation(z_v[:, t, 0:split], dt[t][:, 0:split], ACT.Copy, scale=gs_t[:, t : t + 1])
+            if split < S:
+                nc.vector.tensor_scalar(z_v[:, t, split:S], dt[t][:, split:S], gs_t[:, t : t + 1], None, ALU.mult)
+
+        for n, t in enumerate(ORDER):
+            fetch(t)
+            squares(t)
+            if n >= 1:
+                root(ORDER[n - 1])
+        weigh(ORDER[0])
+        root(ORDER[-1])
+        for t in ORDER[1:]:
+            weigh(t)
 
         ds_g = keep.tile([P, 2 * H], U8, name="ds_g")
         dw_g = keep.tile([P, 2 * H], U32, name="dw_g")
@@ -91,61 +128,51 @@ def tile_picked_daqpolaresa_none_p_kernel(tc, x_words, x_scales, w1, gs, d_words
         nc.vector.tensor_copy(ds_dealt[:].rearrange("p (a t m) -> p a t m", a=2, t=PACK),
                               ds_g[:].rearrange("p (a m t) -> p a t m", a=2, t=PACK))
         for r in range(4):
-            src = 16 * (r // 2) + r % 2
-            nc.sync.dma_start(ds_plane[r:P:32, :].bitcast(I32), ds_dealt[src:P:32, :].bitcast(I32))
+            nc.sync.dma_start(ds_plane[r:P:32, :].bitcast(I32), ds_dealt[8 * r : P : 32, :].bitcast(I32))
         for a, lst in enumerate((ka_l, kb_l)):
             nc.vector.tensor_copy(dw_g[:, a * H : (a + 1) * H], dw_tab[:].bitcast(U32).indirect(lst[:]))
         dw_dealt = keep.tile([P, 2 * H], U32, name="dw_dealt", align_bytes=64)
         nc.vector.tensor_copy(dw_dealt[:].rearrange("p (a t m) -> p a m t", a=2, t=PACK),
                               dw_g[:].rearrange("p (a m t) -> p a m t", a=2, t=PACK))
         nbias = keep.tile([P, PACK], F32, name="nbias")
-        nc.vector.scalar_tensor_tensor(nbias[:], sl_t[:], -1.0, th_t[:], ALU.mult, ALU.mult)
+        slth = keep.tile([P, PACK], F32, name="slth")
+        nc.gpsimd.tensor_tensor(slth[:], sl_t[:], th_t[:], ALU.mult)
+        nc.gpsimd.tensor_scalar(nbias[:], slth[:], -1.0, 0.0, ALU.mult, ALU.add)
 
-        z_planes = keep.tile([P, PACK, S], BF16, name="z_planes")
-        for t in range(PACK):
-            y = keep.tile([P, S], F32, name=f"y{t}")
-            nc.scalar.copy(y[:], y_ps[t][:])
-            pah = keep.tile([P, W], F32, name=f"pah{t}")
-            pb = keep.tile([P, W], F32, name=f"pb{t}")
-            nc.scalar.activation(pah[:], y[:].indirect(n1_l[:]), ACT.Copy, scale=-0.5)
-            nc.scalar.activation(pb[:], y[:].indirect(n2_l[:]), ACT.Copy)
-            dt = keep.tile([P, S], F32, name=f"dt{t}")
-            nc.vector.tensor_tensor(dt[:].indirect(n2_l[:]), pb[:], pah[:], ALU.add)
-            a2 = keep.tile([P, W], F32, name=f"a2{t}")
-            b2 = keep.tile([P, W], F32, name=f"b2{t}")
-            nc.scalar.activation(a2[:], pah[:], ACT.Square, scale=2.0)
-            nc.scalar.activation(b2[:], pb[:], ACT.Square)
-            ss = keep.tile([P, W], F32, name=f"ss{t}")
-            nc.vector.tensor_tensor(ss[:], a2[:], b2[:], ALU.add)
-            ra = keep.tile([P, W], F32, name=f"ra{t}")
-            nc.scalar.activation(ra[:], ss[:], ACT.Sqrt, bias=quarter[:])
-            nc.vector.tensor_copy(dt[:].indirect(n1_l[:]), ra[:])
-            if t < PACK - 1:
-                nc.scalar.activation(z_planes[:, t, :], dt[:], ACT.Copy, scale=gs_t[:, t : t + 1])
-            else:
-                nc.vector.tensor_scalar(z_planes[:, t, :], dt[:], gs_t[:, t : t + 1], None, ALU.mult)
-
-        z_bf = keep.tile([P, S * PACK], BF16, name="z_bf", align_bytes=64)
-        nc.vector.tensor_copy(z_bf[:].rearrange("p (c i t) -> p c t i", i=4, t=PACK),
-                              z_planes[:].rearrange("p t (c i) -> p c t i", i=4))
         z_q = keep.tile([P, S], U32, name="z_q", align_bytes=64)
         z_s = keep.tile([P, S], U8, name="z_s", align_bytes=64)
-        nc.vector.quantize_mx(out=z_q[:].bitcast(FP8X4), scales=z_s[:], in_=z_bf[:])
+        for c in (1, 0):
+            cols = slice(c * W, (c + 1) * W)
+            nc.vector.quantize_mx(out=z_q[:, cols].bitcast(FP8X4), scales=z_s[:, cols], in_=z_bf[:, c * W * PACK : (c + 1) * W * PACK])
 
         out_v = out.rearrange("(p t) j -> t p j", t=PACK)
-        for t in range(PACK):
-            h_ps = psum.tile([P, S], F32, name=f"h_ps{t}")
+        h = [keep.tile([P, S], F32, name=f"h{t}") for t in range(PACK)]
+
+        def product(t, cols, bank, on_scalar=False):
+            h_ps = psum.tile([P, cols.stop - cols.start], F32, name="h_ps", tag=bank)
             for a in range(2):
-                cols = slice(a * H + t * P, a * H + (t + 1) * P)
-                nc.tensor.matmul_mx(out=h_ps[:], lhsT=dw_dealt[:, cols].bitcast(FP8X4), lhsT_scale=ds_plane[:, cols],
-                                    rhs=z_q[:].bitcast(FP8X4), rhs_scale=z_s[:], start=(a == 0), stop=(a == 1))
-            h = keep.tile([P, S], F32, name=f"h{t}")
-            nc.vector.tensor_scalar(h[:], h_ps[:], 0.0625, None, ALU.mult)
+                rows = slice(a * H + t * P, a * H + (t + 1) * P)
+                nc.tensor.matmul_mx(out=h_ps[:], lhsT=dw_dealt[:, rows].bitcast(FP8X4), lhsT_scale=ds_plane[:, rows],
+                                    rhs=z_q[:, cols].bitcast(FP8X4), rhs_scale=z_s[:, cols], start=(a == 0), stop=(a == 1))
+            if on_scalar:
+                nc.scalar.activation(h[t][:, cols], h_ps[:], ACT.Copy, scale=0.0625)
+            else:
+                nc.vector.tensor_scalar(h[t][:, cols], h_ps[:], 0.0625, None, ALU.mult)
+
+        def gate(t):
             sg = keep.tile([P, S], F32, name=f"sg{t}")
             res = keep.tile([P, S], F32, name=f"res{t}")
             for c in range(2):
                 cols = slice(c * W, (c + 1) * W)
-                nc.scalar.activation(sg[:, cols], h[:].indirect(n3_l[:, c * 16 : (c + 1) * 16]), ACT.Sigmoid,
+                nc.scalar.activation(sg[:, cols], h[t][:].indirect(n3_l[:, c * 16 : (c + 1) * 16]), ACT.Sigmoid,
                                      bias=nbias[:, t : t + 1], scale=sl_t[:, t : t + 1])
-            nc.vector.tensor_tensor(res[:], h[:], sg[:], ALU.mult)
-            nc.sync.dma_start(out_v[t], res[:])
+            for cols in ([slice(0, S)] if t < PACK - 1 else [slice(0, W), slice(W, S)]):
+                nc.vector.tensor_tensor(res[:, cols], h[t][:, cols], sg[:, cols], ALU.mult)
+                nc.sync.dma_start(out_v[t][:, cols], res[:, cols])
+
+        product(0, slice(W, S), "bank4", on_scalar=True)
+        product(0, slice(0, W), "bank5")
+        for t in range(1, PACK):
+            product(t, slice(0, S), f"bank{t}")
+            gate(t - 1)
+        gate(PACK - 1)

@@ -4,7 +4,7 @@ import concourse.mybir as mybir
 
 K, T, S, H, W, G = 512, 2048, 512, 512, 256, 2048
 P, PACK = 128, 4
-M_SCALAR = 48
+M_SCALAR = 88
 J_SCALAR = 128
 ORDER = (1, 2, 3, 0)
 FLOPS = 2 * K * H * S * 3
@@ -42,28 +42,28 @@ def tile_picked_daqpolaresa_none_p_kernel(tc, x_words, x_scales, w1, gs, d_words
         ds_plane = keep.tile([P, 2 * H], U8, name="ds_plane", align_bytes=64)
         quarter = keep.tile([P, 1], F32, name="quarter")
         nc.vector.memset(ds_tab[:].bitcast(I32), 0)
-        nc.gpsimd.memset(xs_tab[:].bitcast(I32), 0)
+        nc.vector.memset(xs_tab[:].bitcast(I32), 0)
+        nc.vector.memset(quarter[:], 0.25)
+        nc.vector.memset(ds_plane[:].bitcast(I32), 0)
 
         ka_l = load_list(ka, "ka_l")
         kb_l = load_list(kb, "kb_l")
         nc.sync.dma_start(ds_tab[0:P:8, :].bitcast(I32), d_scales[0].bitcast(I32))
+        for q in range(4):
+            nc.scalar.dma_start(xs_tab[32 * q : 32 * q + 4, :].bitcast(I32), x_scales[0, 4 * q : 4 * q + 4, :].bitcast(I32))
+        offs_l = load_list(offs, "offs_l")
         w_raw = keep.tile([P, PACK, H], F32, name="w_raw")
         nc.sync.dma_start(w_raw[:], w1.rearrange("(p j) i -> p j i", j=PACK))
-        offs_l = load_list(offs, "offs_l")
-        for q in range(4):
-            nc.sync.dma_start(xs_tab[32 * q : 32 * q + 4, :].bitcast(I32), x_scales[0, 4 * q : 4 * q + 4, :].bitcast(I32))
+        n1_l = load_list(n1, "n1_l")
+        n2_l = load_list(n2, "n2_l")
         xw_tab = keep.tile([P, T], I32, name="xw_tab")
         nc.sync.dma_start(xw_tab[:], x_words[0].rearrange("p n t -> p (n t)").bitcast(I32))
         dw_tab = keep.tile([P, G], I32, name="dw_tab")
         nc.sync.dma_start(dw_tab[:], d_words[0].rearrange("p n t -> p (n t)").bitcast(I32))
-        n1_l = load_list(n1, "n1_l")
-        n2_l = load_list(n2, "n2_l")
         gs_t = load_rows(gs, "gs_t")
         sl_t = load_rows(sl, "sl_t")
         th_t = load_rows(th, "th_t")
         n3_l = load_list(n3, "n3_l")
-        nc.gpsimd.memset(quarter[:], 0.25)
-        nc.gpsimd.memset(ds_plane[:].bitcast(I32), 0)
 
         xs_g = keep.tile([P, S], U8, name="xs_g", align_bytes=64)
         nc.vector.tensor_copy(xs_g[:], xs_tab[:].indirect(offs_l[:]))
@@ -83,6 +83,23 @@ def tile_picked_daqpolaresa_none_p_kernel(tc, x_words, x_scales, w1, gs, d_words
             cols = slice(t * P, (t + 1) * P)
             nc.tensor.matmul_mx(out=y_ps[t][:], lhsT=w_q[:, cols].bitcast(FP8X4), lhsT_scale=w_s[:, cols],
                                 rhs=xw_g[:].bitcast(FP8X4), rhs_scale=xs_g[:], start=True, stop=True)
+
+        ds_g = keep.tile([P, 2 * H], U8, name="ds_g")
+        dw_g = keep.tile([P, 2 * H], U32, name="dw_g")
+        for a, lst in enumerate((ka_l, kb_l)):
+            nc.vector.tensor_copy(ds_g[:, a * H : (a + 1) * H], ds_tab[:].indirect(lst[:]))
+        ds_dealt = keep.tile([P, 2 * H], U8, name="ds_dealt")
+        nc.vector.tensor_copy(ds_dealt[:].rearrange("p (a t m) -> p a t m", a=2, t=PACK),
+                              ds_g[:].rearrange("p (a m t) -> p a t m", a=2, t=PACK))
+        for r in range(4):
+            nc.sync.dma_start(ds_plane[r:P:32, :].bitcast(I32), ds_dealt[8 * r : P : 32, :].bitcast(I32))
+        for a, lst in enumerate((ka_l, kb_l)):
+            nc.vector.tensor_copy(dw_g[:, a * H : (a + 1) * H], dw_tab[:].bitcast(U32).indirect(lst[:]))
+        dw_dealt = keep.tile([P, 2 * H], U32, name="dw_dealt", align_bytes=64)
+        nc.vector.tensor_copy(dw_dealt[:].rearrange("p (a t m) -> p a m t", a=2, t=PACK),
+                              dw_g[:].rearrange("p (a m t) -> p a m t", a=2, t=PACK))
+        nbias = keep.tile([P, PACK], F32, name="nbias")
+        nc.vector.scalar_tensor_tensor(nbias[:], sl_t[:], -1.0, th_t[:], ALU.mult, ALU.mult)
 
         z_bf = keep.tile([P, S * PACK], BF16, name="z_bf", align_bytes=64)
         z_v = z_bf[:].rearrange("p (j t) -> p t j", t=PACK)
@@ -108,7 +125,8 @@ def tile_picked_daqpolaresa_none_p_kernel(tc, x_words, x_scales, w1, gs, d_words
             split = J_SCALAR if t == ORDER[-1] else S
             nc.scalar.activation(z_v[:, t, 0:split], dt[t][:, 0:split], ACT.Copy, scale=gs_t[:, t : t + 1])
             if split < S:
-                nc.vector.tensor_scalar(z_v[:, t, split:S], dt[t][:, split:S], gs_t[:, t : t + 1], None, ALU.mult)
+                for lo, hi in ((W, S), (split, W)):
+                    nc.vector.tensor_scalar(z_v[:, t, lo:hi], dt[t][:, lo:hi], gs_t[:, t : t + 1], None, ALU.mult)
 
         for n, t in enumerate(ORDER):
             fetch(t)
@@ -119,25 +137,6 @@ def tile_picked_daqpolaresa_none_p_kernel(tc, x_words, x_scales, w1, gs, d_words
         root(ORDER[-1])
         for t in ORDER[1:]:
             weigh(t)
-
-        ds_g = keep.tile([P, 2 * H], U8, name="ds_g")
-        dw_g = keep.tile([P, 2 * H], U32, name="dw_g")
-        for a, lst in enumerate((ka_l, kb_l)):
-            nc.vector.tensor_copy(ds_g[:, a * H : (a + 1) * H], ds_tab[:].indirect(lst[:]))
-        ds_dealt = keep.tile([P, 2 * H], U8, name="ds_dealt")
-        nc.vector.tensor_copy(ds_dealt[:].rearrange("p (a t m) -> p a t m", a=2, t=PACK),
-                              ds_g[:].rearrange("p (a m t) -> p a t m", a=2, t=PACK))
-        for r in range(4):
-            nc.sync.dma_start(ds_plane[r:P:32, :].bitcast(I32), ds_dealt[8 * r : P : 32, :].bitcast(I32))
-        for a, lst in enumerate((ka_l, kb_l)):
-            nc.vector.tensor_copy(dw_g[:, a * H : (a + 1) * H], dw_tab[:].bitcast(U32).indirect(lst[:]))
-        dw_dealt = keep.tile([P, 2 * H], U32, name="dw_dealt", align_bytes=64)
-        nc.vector.tensor_copy(dw_dealt[:].rearrange("p (a t m) -> p a m t", a=2, t=PACK),
-                              dw_g[:].rearrange("p (a m t) -> p a m t", a=2, t=PACK))
-        nbias = keep.tile([P, PACK], F32, name="nbias")
-        slth = keep.tile([P, PACK], F32, name="slth")
-        nc.gpsimd.tensor_tensor(slth[:], sl_t[:], th_t[:], ALU.mult)
-        nc.gpsimd.tensor_scalar(nbias[:], slth[:], -1.0, 0.0, ALU.mult, ALU.add)
 
         z_q = keep.tile([P, S], U32, name="z_q", align_bytes=64)
         z_s = keep.tile([P, S], U8, name="z_s", align_bytes=64)
@@ -162,11 +161,12 @@ def tile_picked_daqpolaresa_none_p_kernel(tc, x_words, x_scales, w1, gs, d_words
         def gate(t):
             sg = keep.tile([P, S], F32, name=f"sg{t}")
             res = keep.tile([P, S], F32, name=f"res{t}")
-            for c in range(2):
-                cols = slice(c * W, (c + 1) * W)
-                nc.scalar.activation(sg[:, cols], h[t][:].indirect(n3_l[:, c * 16 : (c + 1) * 16]), ACT.Sigmoid,
+            last = t == PACK - 1
+            cuts = (0, 256, 384, S) if last else (0, 256, S)
+            for lo, hi in zip(cuts, cuts[1:]):
+                nc.scalar.activation(sg[:, lo:hi], h[t][:].indirect(n3_l[:, lo // 16 : hi // 16]), ACT.Sigmoid,
                                      bias=nbias[:, t : t + 1], scale=sl_t[:, t : t + 1])
-            for cols in ([slice(0, S)] if t < PACK - 1 else [slice(0, W), slice(W, S)]):
+            for cols in ([slice(lo, hi) for lo, hi in zip(cuts, cuts[1:])] if last else [slice(0, S)]):
                 nc.vector.tensor_tensor(res[:, cols], h[t][:, cols], sg[:, cols], ALU.mult)
                 nc.sync.dma_start(out_v[t][:, cols], res[:, cols])
 

@@ -4,10 +4,11 @@ import concourse.mybir as mybir
 
 K, T, S, H, W, G = 512, 2048, 512, 512, 256, 2048
 P, PACK = 128, 4
-M_SCALAR = 88
-J_SCALAR = 128
-ORDER = (1, 2, 3, 0)
+LIST_COL = 16
 FLOPS = 2 * K * H * S * 3
+
+W_GROUPS_ON_SCALAR = 88
+ORDER = (1, 2, 3, 0)
 
 F32 = mybir.dt.float32
 BF16 = mybir.dt.bfloat16
@@ -65,13 +66,16 @@ def tile_picked_daqpolaresa_none_p_kernel(tc, x_words, x_scales, w1, gs, d_words
         th_t = load_rows(th, "th_t")
         n3_l = load_list(n3, "n3_l")
 
+        warm_sqrt = keep.tile([P, 1], F32, name="warm_sqrt")
+        nc.scalar.activation(warm_sqrt[:], quarter[:], ACT.Sqrt)
+
         xs_g = keep.tile([P, S], U8, name="xs_g", align_bytes=64)
         nc.vector.tensor_copy(xs_g[:], xs_tab[:].indirect(offs_l[:]))
         w_bf = keep.tile([P, H * PACK], BF16, name="w_bf", align_bytes=64)
         w_bf_v = w_bf[:].rearrange("p (t m j) -> p m t j", t=PACK, j=PACK)
         w_raw_v = w_raw[:].rearrange("p j (m t) -> p m t j", t=PACK)
-        nc.scalar.activation(w_bf_v[:, 0:M_SCALAR], w_raw_v[:, 0:M_SCALAR], ACT.Copy)
-        nc.vector.tensor_copy(w_bf_v[:, M_SCALAR:P], w_raw_v[:, M_SCALAR:P])
+        nc.scalar.activation(w_bf_v[:, 0:W_GROUPS_ON_SCALAR], w_raw_v[:, 0:W_GROUPS_ON_SCALAR], ACT.Copy)
+        nc.vector.tensor_copy(w_bf_v[:, W_GROUPS_ON_SCALAR:P], w_raw_v[:, W_GROUPS_ON_SCALAR:P])
         w_q = keep.tile([P, H], U32, name="w_q", align_bytes=64)
         w_s = keep.tile([P, H], U8, name="w_s", align_bytes=64)
         nc.vector.quantize_mx(out=w_q[:].bitcast(FP8X4), scales=w_s[:], in_=w_bf[:])
@@ -80,99 +84,119 @@ def tile_picked_daqpolaresa_none_p_kernel(tc, x_words, x_scales, w1, gs, d_words
 
         y_ps = [psum.tile([P, S], F32, name=f"y_ps{t}", tag=f"bank{t}") for t in range(PACK)]
         for t in ORDER:
-            cols = slice(t * P, (t + 1) * P)
-            nc.tensor.matmul_mx(out=y_ps[t][:], lhsT=w_q[:, cols].bitcast(FP8X4), lhsT_scale=w_s[:, cols],
+            rows = slice(t * P, (t + 1) * P)
+            nc.tensor.matmul_mx(out=y_ps[t][:], lhsT=w_q[:, rows].bitcast(FP8X4), lhsT_scale=w_s[:, rows],
                                 rhs=xw_g[:].bitcast(FP8X4), rhs_scale=xs_g[:], start=True, stop=True)
 
         ds_g = keep.tile([P, 2 * H], U8, name="ds_g")
         dw_g = keep.tile([P, 2 * H], U32, name="dw_g")
-        for a, lst in enumerate((ka_l, kb_l)):
-            nc.vector.tensor_copy(ds_g[:, a * H : (a + 1) * H], ds_tab[:].indirect(lst[:]))
+        for a, codes in enumerate((ka_l, kb_l)):
+            nc.vector.tensor_copy(ds_g[:, a * H : (a + 1) * H], ds_tab[:].indirect(codes[:]))
         ds_dealt = keep.tile([P, 2 * H], U8, name="ds_dealt")
         nc.vector.tensor_copy(ds_dealt[:].rearrange("p (a t m) -> p a t m", a=2, t=PACK),
                               ds_g[:].rearrange("p (a m t) -> p a t m", a=2, t=PACK))
         for r in range(4):
             nc.sync.dma_start(ds_plane[r:P:32, :].bitcast(I32), ds_dealt[8 * r : P : 32, :].bitcast(I32))
-        for a, lst in enumerate((ka_l, kb_l)):
-            nc.vector.tensor_copy(dw_g[:, a * H : (a + 1) * H], dw_tab[:].bitcast(U32).indirect(lst[:]))
+        for a, codes in enumerate((ka_l, kb_l)):
+            nc.vector.tensor_copy(dw_g[:, a * H : (a + 1) * H], dw_tab[:].bitcast(U32).indirect(codes[:]))
         dw_dealt = keep.tile([P, 2 * H], U32, name="dw_dealt", align_bytes=64)
         nc.vector.tensor_copy(dw_dealt[:].rearrange("p (a t m) -> p a m t", a=2, t=PACK),
                               dw_g[:].rearrange("p (a m t) -> p a m t", a=2, t=PACK))
-        nbias = keep.tile([P, PACK], F32, name="nbias")
-        nc.vector.scalar_tensor_tensor(nbias[:], sl_t[:], -1.0, th_t[:], ALU.mult, ALU.mult)
+        sg_bias = keep.tile([P, PACK], F32, name="sg_bias")
+        nc.vector.scalar_tensor_tensor(sg_bias[:], sl_t[:], -1.0, th_t[:], ALU.mult, ALU.mult)
 
         z_bf = keep.tile([P, S * PACK], BF16, name="z_bf", align_bytes=64)
         z_v = z_bf[:].rearrange("p (j t) -> p t j", t=PACK)
-        y, pah, pb, a2, b2, ss, ra, dt = ([keep.tile([P, n], F32, name=f"{name}{t}") for t in range(PACK)]
-            for name, n in (("y", S), ("pah", W), ("pb", W), ("a2", W), ("b2", W), ("ss", W), ("ra", W), ("dt", S)))
+        h = [keep.tile([P, 2 * S if t < PACK - 1 else S], F32, name=f"h{t}") for t in range(PACK)]
+        sq_narrow = keep.tile([P, S], F32, name="sq_narrow")
+        sq = [h[t][:, S : 2 * S] if t < PACK - 1 else sq_narrow[:] for t in range(PACK)]
+        y, pa_half, pb, sq_sum, ra, dt = (
+            [keep.tile([P, width], F32, name=f"{name}{t}") for t in range(PACK)]
+            for name, width in (("y", S), ("pa_half", W), ("pb", W), ("sq_sum", W), ("ra", W), ("dt", S))
+        )
 
-        def fetch(t):
+        def empty_bank(t):
             nc.scalar.copy(y[t][:], y_ps[t][:])
-            nc.scalar.activation(pah[t][:], y[t][:].indirect(n1_l[:]), ACT.Copy, scale=-0.5)
+
+        def fetch_pairs(t):
+            nc.scalar.activation(pa_half[t][:], y[t][:].indirect(n1_l[:]), ACT.Copy, scale=-0.5)
             nc.scalar.activation(pb[t][:], y[t][:].indirect(n2_l[:]), ACT.Copy)
-            nc.vector.tensor_tensor(dt[t][:].indirect(n2_l[:]), pb[t][:], pah[t][:], ALU.add)
+            nc.vector.tensor_tensor(dt[t][:].indirect(n2_l[:]), pb[t][:], pa_half[t][:], ALU.add)
 
-        def squares(t):
-            nc.scalar.activation(a2[t][:], pah[t][:], ACT.Square, scale=2.0)
-            nc.scalar.activation(b2[t][:], pb[t][:], ACT.Square)
-            nc.vector.tensor_tensor(ss[t][:], a2[t][:], b2[t][:], ALU.add)
+        def add_squares(t):
+            nc.scalar.activation(sq[t][:, 0:W], pa_half[t][:], ACT.Square, scale=2.0)
+            nc.scalar.activation(sq[t][:, W:S], pb[t][:], ACT.Square)
+            nc.vector.tensor_tensor(sq_sum[t][:], sq[t][:, 0:W], sq[t][:, W:S], ALU.add)
 
-        def root(t):
-            nc.scalar.activation(ra[t][:], ss[t][:], ACT.Sqrt, bias=quarter[:])
+        def put_root(t):
+            nc.scalar.activation(ra[t][:], sq_sum[t][:], ACT.Sqrt, bias=quarter[:])
             nc.vector.tensor_copy(dt[t][:].indirect(n1_l[:]), ra[t][:])
 
-        def weigh(t):
-            split = J_SCALAR if t == ORDER[-1] else S
-            nc.scalar.activation(z_v[:, t, 0:split], dt[t][:, 0:split], ACT.Copy, scale=gs_t[:, t : t + 1])
-            if split < S:
-                for lo, hi in ((W, S), (split, W)):
-                    nc.vector.tensor_scalar(z_v[:, t, lo:hi], dt[t][:, lo:hi], gs_t[:, t : t + 1], None, ALU.mult)
+        def weigh_on_scalar(t, width):
+            nc.scalar.activation(z_v[:, t, 0:width], dt[t][:, 0:width], ACT.Copy, scale=gs_t[:, t : t + 1])
 
+        empty_bank(ORDER[0])
+        empty_bank(ORDER[1])
         for n, t in enumerate(ORDER):
-            fetch(t)
-            squares(t)
+            fetch_pairs(t)
+            add_squares(t)
             if n >= 1:
-                root(ORDER[n - 1])
-        weigh(ORDER[0])
-        root(ORDER[-1])
-        for t in ORDER[1:]:
-            weigh(t)
+                put_root(ORDER[n - 1])
+            if n + 2 < PACK:
+                empty_bank(ORDER[n + 2])
+        last_tile = ORDER[-1]
+        weigh_on_scalar(ORDER[0], S)
+        weigh_on_scalar(ORDER[1], S)
+        put_root(last_tile)
+        weigh_on_scalar(ORDER[2], S)
+        weigh_on_scalar(last_tile, P)
+
+        warm_sigmoid = keep.tile([P, 1], F32, name="warm_sigmoid")
+        nc.scalar.activation(warm_sigmoid[:], dt[last_tile][:, 0:1], ACT.Sigmoid)
 
         z_q = keep.tile([P, S], U32, name="z_q", align_bytes=64)
         z_s = keep.tile([P, S], U8, name="z_s", align_bytes=64)
-        for c in (1, 0):
-            cols = slice(c * W, (c + 1) * W)
-            nc.vector.quantize_mx(out=z_q[:, cols].bitcast(FP8X4), scales=z_s[:, cols], in_=z_bf[:, c * W * PACK : (c + 1) * W * PACK])
+
+        def weigh_on_vector(c):
+            cols = slice(c * P, (c + 1) * P)
+            nc.vector.tensor_scalar(z_v[:, last_tile, cols], dt[last_tile][:, cols], gs_t[:, last_tile : last_tile + 1], None, ALU.mult)
+
+        def quantize_z(c):
+            cols = slice(c * P, (c + 1) * P)
+            nc.vector.quantize_mx(out=z_q[:, cols].bitcast(FP8X4), scales=z_s[:, cols], in_=z_bf[:, c * P * PACK : (c + 1) * P * PACK])
+
+        weigh_on_vector(3)
+        for c in (3, 2):
+            weigh_on_vector(c - 1)
+            quantize_z(c)
+        quantize_z(1)
+        quantize_z(0)
 
         out_v = out.rearrange("(p t) j -> t p j", t=PACK)
-        h = [keep.tile([P, S], F32, name=f"h{t}") for t in range(PACK)]
 
-        def product(t, cols, bank, on_scalar=False):
+        def second_product(t, cols, bank):
             h_ps = psum.tile([P, cols.stop - cols.start], F32, name="h_ps", tag=bank)
             for a in range(2):
                 rows = slice(a * H + t * P, a * H + (t + 1) * P)
                 nc.tensor.matmul_mx(out=h_ps[:], lhsT=dw_dealt[:, rows].bitcast(FP8X4), lhsT_scale=ds_plane[:, rows],
                                     rhs=z_q[:, cols].bitcast(FP8X4), rhs_scale=z_s[:, cols], start=(a == 0), stop=(a == 1))
-            if on_scalar:
-                nc.scalar.activation(h[t][:, cols], h_ps[:], ACT.Copy, scale=0.0625)
-            else:
-                nc.vector.tensor_scalar(h[t][:, cols], h_ps[:], 0.0625, None, ALU.mult)
+            nc.vector.tensor_scalar(h[t][:, cols], h_ps[:], 0.0625, None, ALU.mult)
 
-        def gate(t):
+        def gate_and_store(t):
             sg = keep.tile([P, S], F32, name=f"sg{t}")
             res = keep.tile([P, S], F32, name=f"res{t}")
-            last = t == PACK - 1
-            cuts = (0, 256, 384, S) if last else (0, 256, S)
-            for lo, hi in zip(cuts, cuts[1:]):
-                nc.scalar.activation(sg[:, lo:hi], h[t][:].indirect(n3_l[:, lo // 16 : hi // 16]), ACT.Sigmoid,
-                                     bias=nbias[:, t : t + 1], scale=sl_t[:, t : t + 1])
-            for cols in ([slice(lo, hi) for lo, hi in zip(cuts, cuts[1:])] if last else [slice(0, S)]):
-                nc.vector.tensor_tensor(res[:, cols], h[t][:, cols], sg[:, cols], ALU.mult)
-                nc.sync.dma_start(out_v[t][:, cols], res[:, cols])
+            cuts = (0, S // 2, 3 * S // 4, S) if t == PACK - 1 else (0, S)
+            pieces = list(zip(cuts, cuts[1:]))
+            for lo, hi in pieces:
+                nc.scalar.activation(sg[:, lo:hi], h[t][:].indirect(n3_l[:, lo // LIST_COL : hi // LIST_COL]), ACT.Sigmoid,
+                                     bias=sg_bias[:, t : t + 1], scale=sl_t[:, t : t + 1])
+            for lo, hi in pieces:
+                nc.vector.tensor_tensor(res[:, lo:hi], h[t][:, lo:hi], sg[:, lo:hi], ALU.mult)
+                nc.sync.dma_start(out_v[t][:, lo:hi], res[:, lo:hi])
 
-        product(0, slice(W, S), "bank4", on_scalar=True)
-        product(0, slice(0, W), "bank5")
+        for c in (3, 2, 1, 0):
+            second_product(0, slice(c * P, (c + 1) * P), f"bank{PACK + c}")
         for t in range(1, PACK):
-            product(t, slice(0, S), f"bank{t}")
-            gate(t - 1)
-        gate(PACK - 1)
+            second_product(t, slice(0, S), f"bank{t}")
+            gate_and_store(t - 1)
+        gate_and_store(PACK - 1)

from contextlib import ExitStack

import concourse.mybir as mybir

K, T, S, H, W, G = 512, 2048, 512, 512, 256, 2048
P, PACK = 128, 4
LIST_COL = 16
FLOPS = 2 * K * H * S * 3

W_GROUPS_ON_SCALAR = 88
ORDER = (1, 2, 3, 0)

F32 = mybir.dt.float32
BF16 = mybir.dt.bfloat16
I32 = mybir.dt.int32
U32 = mybir.dt.uint32
U16 = mybir.dt.uint16
U8 = mybir.dt.uint8
FP8X4 = mybir.dt.float8_e4m3fn_x4
ACT = mybir.ActivationFunctionType
ALU = mybir.AluOpType


def tile_picked_daqpolaresa_none_p_kernel(tc, x_words, x_scales, w1, gs, d_words, d_scales, sl, th, offs, n1, n2, ka, kb, n3, out):
    nc = tc.nc
    with ExitStack() as ctx:
        lists = ctx.enter_context(tc.tile_pool(name="lists", bufs=1))
        keep = ctx.enter_context(tc.tile_pool(name="keep", bufs=1))
        psum = ctx.enter_context(tc.psum_pool(name="psum", bufs=1))

        def load_list(src, name):
            tile = lists.tile(list(src.shape), U16, name=name)
            nc.sync.dma_start(tile[:], src)
            return tile

        def load_rows(src, name):
            tile = keep.tile([P, PACK], F32, name=name)
            nc.sync.dma_start(tile[:], src.rearrange("(p t) o -> p (t o)", t=PACK))
            return tile

        xs_tab = keep.tile([P, T], U8, name="xs_tab")
        ds_tab = keep.tile([P, G], U8, name="ds_tab")
        ds_plane = keep.tile([P, 2 * H], U8, name="ds_plane", align_bytes=64)
        quarter = keep.tile([P, 1], F32, name="quarter")
        nc.vector.memset(ds_tab[:].bitcast(I32), 0)
        nc.vector.memset(xs_tab[:].bitcast(I32), 0)
        nc.vector.memset(quarter[:], 0.25)
        nc.vector.memset(ds_plane[:].bitcast(I32), 0)

        ka_l = load_list(ka, "ka_l")
        kb_l = load_list(kb, "kb_l")
        nc.sync.dma_start(ds_tab[0:P:8, :].bitcast(I32), d_scales[0].bitcast(I32))
        for q in range(4):
            nc.scalar.dma_start(xs_tab[32 * q : 32 * q + 4, :].bitcast(I32), x_scales[0, 4 * q : 4 * q + 4, :].bitcast(I32))
        offs_l = load_list(offs, "offs_l")
        w_raw = keep.tile([P, PACK, H], F32, name="w_raw")
        nc.sync.dma_start(w_raw[:], w1.rearrange("(p j) i -> p j i", j=PACK))
        n1_l = load_list(n1, "n1_l")
        n2_l = load_list(n2, "n2_l")
        xw_tab = keep.tile([P, T], I32, name="xw_tab")
        nc.sync.dma_start(xw_tab[:], x_words[0].rearrange("p n t -> p (n t)").bitcast(I32))
        dw_tab = keep.tile([P, G], I32, name="dw_tab")
        nc.sync.dma_start(dw_tab[:], d_words[0].rearrange("p n t -> p (n t)").bitcast(I32))
        gs_t = load_rows(gs, "gs_t")
        sl_t = load_rows(sl, "sl_t")
        th_t = load_rows(th, "th_t")
        n3_l = load_list(n3, "n3_l")

        warm_sqrt = keep.tile([P, 1], F32, name="warm_sqrt")
        nc.scalar.activation(warm_sqrt[:], quarter[:], ACT.Sqrt)

        xs_g = keep.tile([P, S], U8, name="xs_g", align_bytes=64)
        nc.vector.tensor_copy(xs_g[:], xs_tab[:].indirect(offs_l[:]))
        w_bf = keep.tile([P, H * PACK], BF16, name="w_bf", align_bytes=64)
        w_bf_v = w_bf[:].rearrange("p (t m j) -> p m t j", t=PACK, j=PACK)
        w_raw_v = w_raw[:].rearrange("p j (m t) -> p m t j", t=PACK)
        nc.scalar.activation(w_bf_v[:, 0:W_GROUPS_ON_SCALAR], w_raw_v[:, 0:W_GROUPS_ON_SCALAR], ACT.Copy)
        nc.vector.tensor_copy(w_bf_v[:, W_GROUPS_ON_SCALAR:P], w_raw_v[:, W_GROUPS_ON_SCALAR:P])
        w_q = keep.tile([P, H], U32, name="w_q", align_bytes=64)
        w_s = keep.tile([P, H], U8, name="w_s", align_bytes=64)
        nc.vector.quantize_mx(out=w_q[:].bitcast(FP8X4), scales=w_s[:], in_=w_bf[:])
        xw_g = keep.tile([P, S], U32, name="xw_g", align_bytes=64)
        nc.vector.tensor_copy(xw_g[:], xw_tab[:].bitcast(U32).indirect(offs_l[:]))

        y_ps = [psum.tile([P, S], F32, name=f"y_ps{t}", tag=f"bank{t}") for t in range(PACK)]
        for t in ORDER:
            rows = slice(t * P, (t + 1) * P)
            nc.tensor.matmul_mx(out=y_ps[t][:], lhsT=w_q[:, rows].bitcast(FP8X4), lhsT_scale=w_s[:, rows],
                                rhs=xw_g[:].bitcast(FP8X4), rhs_scale=xs_g[:], start=True, stop=True)

        ds_g = keep.tile([P, 2 * H], U8, name="ds_g")
        dw_g = keep.tile([P, 2 * H], U32, name="dw_g")
        for a, codes in enumerate((ka_l, kb_l)):
            nc.vector.tensor_copy(ds_g[:, a * H : (a + 1) * H], ds_tab[:].indirect(codes[:]))
        ds_dealt = keep.tile([P, 2 * H], U8, name="ds_dealt")
        nc.vector.tensor_copy(ds_dealt[:].rearrange("p (a t m) -> p a t m", a=2, t=PACK),
                              ds_g[:].rearrange("p (a m t) -> p a t m", a=2, t=PACK))
        for r in range(4):
            nc.sync.dma_start(ds_plane[r:P:32, :].bitcast(I32), ds_dealt[8 * r : P : 32, :].bitcast(I32))
        for a, codes in enumerate((ka_l, kb_l)):
            nc.vector.tensor_copy(dw_g[:, a * H : (a + 1) * H], dw_tab[:].bitcast(U32).indirect(codes[:]))
        dw_dealt = keep.tile([P, 2 * H], U32, name="dw_dealt", align_bytes=64)
        nc.vector.tensor_copy(dw_dealt[:].rearrange("p (a t m) -> p a m t", a=2, t=PACK),
                              dw_g[:].rearrange("p (a m t) -> p a m t", a=2, t=PACK))
        sg_bias = keep.tile([P, PACK], F32, name="sg_bias")
        nc.vector.scalar_tensor_tensor(sg_bias[:], sl_t[:], -1.0, th_t[:], ALU.mult, ALU.mult)

        z_bf = keep.tile([P, S * PACK], BF16, name="z_bf", align_bytes=64)
        z_v = z_bf[:].rearrange("p (j t) -> p t j", t=PACK)
        h = [keep.tile([P, 2 * S if t < PACK - 1 else S], F32, name=f"h{t}") for t in range(PACK)]
        sq_narrow = keep.tile([P, S], F32, name="sq_narrow")
        sq = [h[t][:, S : 2 * S] if t < PACK - 1 else sq_narrow[:] for t in range(PACK)]
        y, pa_half, pb, sq_sum, ra, dt = (
            [keep.tile([P, width], F32, name=f"{name}{t}") for t in range(PACK)]
            for name, width in (("y", S), ("pa_half", W), ("pb", W), ("sq_sum", W), ("ra", W), ("dt", S))
        )

        def empty_bank(t):
            nc.scalar.copy(y[t][:], y_ps[t][:])

        def fetch_pairs(t):
            nc.scalar.activation(pa_half[t][:], y[t][:].indirect(n1_l[:]), ACT.Copy, scale=-0.5)
            nc.scalar.activation(pb[t][:], y[t][:].indirect(n2_l[:]), ACT.Copy)
            nc.vector.tensor_tensor(dt[t][:].indirect(n2_l[:]), pb[t][:], pa_half[t][:], ALU.add)

        def add_squares(t):
            nc.scalar.activation(sq[t][:, 0:W], pa_half[t][:], ACT.Square, scale=2.0)
            nc.scalar.activation(sq[t][:, W:S], pb[t][:], ACT.Square)
            nc.vector.tensor_tensor(sq_sum[t][:], sq[t][:, 0:W], sq[t][:, W:S], ALU.add)

        def put_root(t):
            nc.scalar.activation(ra[t][:], sq_sum[t][:], ACT.Sqrt, bias=quarter[:])
            nc.vector.tensor_copy(dt[t][:].indirect(n1_l[:]), ra[t][:])

        def weigh_on_scalar(t, width):
            nc.scalar.activation(z_v[:, t, 0:width], dt[t][:, 0:width], ACT.Copy, scale=gs_t[:, t : t + 1])

        empty_bank(ORDER[0])
        empty_bank(ORDER[1])
        for n, t in enumerate(ORDER):
            fetch_pairs(t)
            add_squares(t)
            if n >= 1:
                put_root(ORDER[n - 1])
            if n + 2 < PACK:
                empty_bank(ORDER[n + 2])
        last_tile = ORDER[-1]
        weigh_on_scalar(ORDER[0], S)
        weigh_on_scalar(ORDER[1], S)
        put_root(last_tile)
        weigh_on_scalar(ORDER[2], S)
        weigh_on_scalar(last_tile, P)

        warm_sigmoid = keep.tile([P, 1], F32, name="warm_sigmoid")
        nc.scalar.activation(warm_sigmoid[:], dt[last_tile][:, 0:1], ACT.Sigmoid)

        z_q = keep.tile([P, S], U32, name="z_q", align_bytes=64)
        z_s = keep.tile([P, S], U8, name="z_s", align_bytes=64)

        def weigh_on_vector(c):
            cols = slice(c * P, (c + 1) * P)
            nc.vector.tensor_scalar(z_v[:, last_tile, cols], dt[last_tile][:, cols], gs_t[:, last_tile : last_tile + 1], None, ALU.mult)

        def quantize_z(c):
            cols = slice(c * P, (c + 1) * P)
            nc.vector.quantize_mx(out=z_q[:, cols].bitcast(FP8X4), scales=z_s[:, cols], in_=z_bf[:, c * P * PACK : (c + 1) * P * PACK])

        weigh_on_vector(3)
        for c in (3, 2):
            weigh_on_vector(c - 1)
            quantize_z(c)
        quantize_z(1)
        quantize_z(0)

        out_v = out.rearrange("(p t) j -> t p j", t=PACK)

        def second_product(t, cols, bank):
            h_ps = psum.tile([P, cols.stop - cols.start], F32, name="h_ps", tag=bank)
            for a in range(2):
                rows = slice(a * H + t * P, a * H + (t + 1) * P)
                nc.tensor.matmul_mx(out=h_ps[:], lhsT=dw_dealt[:, rows].bitcast(FP8X4), lhsT_scale=ds_plane[:, rows],
                                    rhs=z_q[:, cols].bitcast(FP8X4), rhs_scale=z_s[:, cols], start=(a == 0), stop=(a == 1))
            nc.vector.tensor_scalar(h[t][:, cols], h_ps[:], 0.0625, None, ALU.mult)

        def gate_and_store(t):
            sg = keep.tile([P, S], F32, name=f"sg{t}")
            res = keep.tile([P, S], F32, name=f"res{t}")
            cuts = (0, S // 2, 3 * S // 4, S) if t == PACK - 1 else (0, S)
            pieces = list(zip(cuts, cuts[1:]))
            for lo, hi in pieces:
                nc.scalar.activation(sg[:, lo:hi], h[t][:].indirect(n3_l[:, lo // LIST_COL : hi // LIST_COL]), ACT.Sigmoid,
                                     bias=sg_bias[:, t : t + 1], scale=sl_t[:, t : t + 1])
            for lo, hi in pieces:
                nc.vector.tensor_tensor(res[:, lo:hi], h[t][:, lo:hi], sg[:, lo:hi], ALU.mult)
                nc.sync.dma_start(out_v[t][:, lo:hi], res[:, lo:hi])

        for c in (3, 2, 1, 0):
            second_product(0, slice(c * P, (c + 1) * P), f"bank{PACK + c}")
        for t in range(1, PACK):
            second_product(t, slice(0, S), f"bank{t}")
            gate_and_store(t - 1)
        gate_and_store(PACK - 1)
